import numpy as np
CORES = [0,1,2,3,4,5,6,7]
N = 8
def setup_inputs(rng):
    return {"x": rng.standard_normal((N, 128, 1024), dtype=np.float32)}
def reference(x):
    s = x.sum(axis=0, dtype=np.float64).astype(x.dtype)
    s = np.maximum(s, 0)
    return {"y": np.broadcast_to(s, (N,) + s.shape)}

from concourse.bass import DstId, RemoteDMATransfer
from concourse.mybir import AluOpType

N = 8
B = 128

SCRATCH = {
    "xs":   ("sbuf", [128, N * B], "float32"),
    "land": ("sbuf", [128, (N - 1) * B], "float32"),
    "t1":   ("sbuf", [128, 4 * B], "float32"),
    "t2":   ("sbuf", [128, 2 * B], "float32"),
    "t3":   ("sbuf", [128, B], "float32"),
    "zero": ("sbuf", [128, B], "float32"),
    "out":  ("sbuf", [128, N * B], "float32"),
}
SEMAPHORES = ["loaded", "part", "full", "sent", "vdone", "stored"]


def rank_program(g, core, T, topo):
    r = T.rank_of(core)
    if r is None:
        return
    sem = T.sem
    v = g.vector
    peers = [j for j in range(N) if j != r]

    def dst_id(rank):
        rid, pid, sengine = topo.addr(T.cores[rank])
        return DstId(rid=rid, pnc=pid)

    def blk(j):
        return slice(j * B, (j + 1) * B)

    g.dma_start(T.xs[:], T.x[:]).then_inc(sem.loaded, 16)
    v.memset(T.zero[:], 0.0).then_inc(sem.vdone, 1)
    g.wait_ge(sem.loaded, 16)

    g.remote_dma_fused(
        [
            RemoteDMATransfer(
                dst_ids=[dst_id(j)],
                dma_engine_mask=0x3 << (2 * i),
                remote_sem=sem.part,
                src=T.xs[:, blk(j)],
                dst=T.land[:, blk((r - j - 1) % N)],
            )
            for i, j in enumerate(peers)
        ],
        local_sem=sem.sent,
    )

    v.wait_ge(sem.part, 2 * (N - 1))
    v.wait_ge(sem.loaded, 16)
    v.tensor_tensor(T.t1[:, 0:3 * B], T.land[:, 0:3 * B], T.land[:, 3 * B:6 * B], AluOpType.add).then_inc(sem.vdone, 1)
    v.tensor_tensor(T.t1[:, 3 * B:4 * B], T.land[:, 6 * B:7 * B], T.xs[:, blk(r)], AluOpType.add).then_inc(sem.vdone, 1)
    v.wait_ge(sem.vdone, 3)
    v.tensor_tensor(T.t2[:], T.t1[:, 0:2 * B], T.t1[:, 2 * B:4 * B], AluOpType.add).then_inc(sem.vdone, 1)
    v.wait_ge(sem.vdone, 4)
    v.tensor_tensor(T.t3[:], T.t2[:, 0:B], T.t2[:, B:2 * B], AluOpType.add).then_inc(sem.vdone, 1)
    v.wait_ge(sem.vdone, 5)
    v.tensor_tensor(T.out[:, blk(r)], T.t3[:], T.zero[:], AluOpType.max).then_inc(sem.vdone, 1)

    g.wait_ge(sem.vdone, 6)
    g.remote_dma_fused(
        [
            RemoteDMATransfer(
                dst_ids=[dst_id(j) for j in peers],
                dma_engine_mask=0xFFFF,
                remote_sem=sem.full,
                srcs=[T.out[:, blk(r)]],
                dsts=[T.out[:, blk(r)] for j in peers],
            )
        ],
        local_sem=sem.sent,
    )

    g.wait_ge(sem.full, 16 * (N - 1))
    g.dma_start(T.y[:], T.out[:]).then_inc(sem.stored, 16)
    g.wait_ge(sem.stored, 16)
    g.wait_ge(sem.sent, 2 * (N - 1) + 16)
